import numpy as np
import ml_dtypes

BF16 = ml_dtypes.bfloat16


def bf(x):
    return np.asarray(x, np.float32).astype(BF16)


def f32(x):
    return np.asarray(x, np.float32)


def f64(x):
    return np.asarray(x).astype(np.float64)


def striped(idx):
    return np.concatenate([l.reshape(-1, 16).T for l in idx])


def rows(idx, k):
    return np.tile(np.repeat(idx, 16, axis=0), (k // (16 * 8), 1))


def look(tab, idx):
    return np.take_along_axis(f64(tab), rows(idx, len(tab)), axis=1)


K, S, H, D, V, N = 128, 2048, 256, 2, 1024, 2048


def setup_inputs():
    return {"z": bf(np.random.standard_normal((H, S))), "wt": bf(np.random.standard_normal((H, K)) / np.sqrt(H)), "x0": f32(1.0 * np.random.standard_normal((K, V))), "offs": striped(np.stack([np.random.permutation(S)[:N] for _ in range(8)]))}


def reference(z, wt, x0, offs):
    idx = np.stack([g.T.reshape(-1) for g in np.split(offs, 8)])
    tab = f64(wt).T @ f64(z)
    x = f64(x0)
    for d in range(D):
        x = np.maximum(x, look(tab, idx[:, d * V:(d + 1) * V]))
    return x

@@ -1,0 +1,60 @@
+import concourse.mybir as mybir
+
+P = 128
+K = 256
+S = 2048
+V = 1024
+D = 2
+CHUNK = 512
+PIECE = 512
+FLOPS = 2 * P * K * S
+
+BF16, F32, U16 = mybir.dt.bfloat16, mybir.dt.float32, mybir.dt.uint16
+MAX = mybir.AluOpType.max
+
+
+def tile_lookup_pjmax_out_kernel(tc, z, wt, x0, offs, out):
+    nc = tc.nc
+    halves = K // P
+    z_by_feature = z.rearrange("(p c) s -> p c s", c=halves)
+    wt_by_feature = wt.rearrange("(p c) r -> p c r", c=halves)
+
+    with (
+        tc.tile_pool(name="held", bufs=1) as held,
+        tc.psum_pool(name="psum", bufs=1) as psum,
+    ):
+        offsets = held.tile([P, D * V // 16], U16, name="offsets")
+        weights = held.tile([P, halves, P], BF16, name="weights")
+        table = held.tile([P, S], F32, name="table")
+        own = held.tile([P, V], F32, name="own")
+
+        nc.scalar.dma_start(weights[:], wt_by_feature)
+        z_chunks = []
+        for c in range(S // CHUNK):
+            z_chunk = held.tile([P, halves, CHUNK], BF16, name=f"z_chunk{c}")
+            queue = nc.sync if c % 2 == 0 else nc.scalar
+            queue.dma_start(z_chunk[:], z_by_feature[:, :, c * CHUNK : (c + 1) * CHUNK])
+            z_chunks.append(z_chunk)
+        nc.sync.dma_start(offsets[:], offs)
+        nc.sync.dma_start(own[:], x0)
+
+        for c, z_chunk in enumerate(z_chunks):
+            bank = psum.tile([P, CHUNK], F32, name=f"bank{c}")
+            for h in range(halves):
+                nc.tensor.matmul(bank[:], weights[:, h, :], z_chunk[:, h, :], start=h == 0, stop=h == halves - 1)
+            columns = table[:, c * CHUNK : (c + 1) * CHUNK]
+            if c % 2 == 0:
+                nc.scalar.copy(columns, bank[:])
+            else:
+                nc.vector.tensor_copy(columns, bank[:])
+
+        for j in range(0, V, PIECE):
+            largest = own[:, j : j + PIECE]
+            for n in range(D):
+                first = (V * n + j) // 16
+                larger = held.tile([P, PIECE], F32, name=f"larger{j}_{n}")
+                nc.vector.tensor_tensor(
+                    larger[:], table[:].indirect(offsets[:, first : first + PIECE // 16]), largest, MAX
+                )
+                largest = larger[:]
+            nc.sync.dma_start(out[:, j : j + PIECE], largest)

@@ -7,6 +7,7 @@ V = 1024
 D = 2
 CHUNK = 512
 PIECE = 512
+WARM_UPS = 5
 FLOPS = 2 * P * K * S
 
 BF16, F32, U16 = mybir.dt.bfloat16, mybir.dt.float32, mybir.dt.uint16
@@ -38,8 +39,14 @@ def tile_lookup_pjmax_out_kernel(tc, z, wt, x0, offs, out):
         nc.sync.dma_start(offsets[:], offs)
         nc.sync.dma_start(own[:], x0)
 
+        banks = [psum.tile([P, CHUNK], F32, name=f"bank{c}") for c in range(S // CHUNK)]
+        zeros = held.tile([P, CHUNK], BF16, name="zeros")
+        nc.vector.memset(zeros[:], 0.0)
+        for w in range(WARM_UPS):
+            nc.tensor.matmul(banks[-1][:], zeros[:, :P], zeros[:], start=True, stop=True)
+
         for c, z_chunk in enumerate(z_chunks):
-            bank = psum.tile([P, CHUNK], F32, name=f"bank{c}")
+            bank = banks[c]
             for h in range(halves):
                 nc.tensor.matmul(bank[:], weights[:, h, :], z_chunk[:, h, :], start=h == 0, stop=h == halves - 1)
             columns = table[:, c * CHUNK : (c + 1) * CHUNK]

@@ -5,9 +5,10 @@ K = 256
 S = 2048
 V = 1024
 D = 2
-CHUNK = 512
+LOAD = 512
+BLOCK = 256
 PIECE = 512
-WARM_UPS = 5
+WARM_UPS = 16
 FLOPS = 2 * P * K * S
 
 BF16, F32, U16 = mybir.dt.bfloat16, mybir.dt.float32, mybir.dt.uint16
@@ -27,41 +28,48 @@ def tile_lookup_pjmax_out_kernel(tc, z, wt, x0, offs, out):
         offsets = held.tile([P, D * V // 16], U16, name="offsets")
         weights = held.tile([P, halves, P], BF16, name="weights")
         table = held.tile([P, S], F32, name="table")
-        own = held.tile([P, V], F32, name="own")
+        own = [held.tile([P, PIECE], F32, name=f"own{j}") for j in range(V // PIECE)]
+        zeros = held.tile([P, P], BF16, name="zeros")
+        z_chunks = [held.tile([P, halves, LOAD], BF16, name=f"z_chunk{c}") for c in range(S // LOAD)]
+        banks = [psum.tile([P, BLOCK], F32, name=f"bank{b}") for b in range(S // BLOCK)]
 
         nc.scalar.dma_start(weights[:], wt_by_feature)
-        z_chunks = []
-        for c in range(S // CHUNK):
-            z_chunk = held.tile([P, halves, CHUNK], BF16, name=f"z_chunk{c}")
-            queue = nc.sync if c % 2 == 0 else nc.scalar
-            queue.dma_start(z_chunk[:], z_by_feature[:, :, c * CHUNK : (c + 1) * CHUNK])
-            z_chunks.append(z_chunk)
-        nc.sync.dma_start(offsets[:], offs)
-        nc.sync.dma_start(own[:], x0)
-
-        banks = [psum.tile([P, CHUNK], F32, name=f"bank{c}") for c in range(S // CHUNK)]
-        zeros = held.tile([P, CHUNK], BF16, name="zeros")
-        nc.vector.memset(zeros[:], 0.0)
-        for w in range(WARM_UPS):
-            nc.tensor.matmul(banks[-1][:], zeros[:, :P], zeros[:], start=True, stop=True)
-
         for c, z_chunk in enumerate(z_chunks):
-            bank = banks[c]
+            queue = nc.sync if c % 2 == 0 else nc.scalar
+            queue.dma_start(z_chunk[:], z_by_feature[:, :, c * LOAD : (c + 1) * LOAD])
+        nc.sync.dma_start(offsets[:], offs)
+        for j, own_part in enumerate(own):
+            queue = nc.scalar if j % 2 == 0 else nc.sync
+            queue.dma_start(own_part[:], x0[:, j * PIECE : (j + 1) * PIECE])
+
+        nc.gpsimd.memset(zeros[:], 0.0)
+        for w in range(WARM_UPS):
+            nc.tensor.matmul(banks[-1][:, :P], zeros[:], zeros[:], start=True, stop=True)
+
+        for b, bank in enumerate(banks):
+            z_chunk = z_chunks[b * BLOCK // LOAD]
+            first = b * BLOCK % LOAD
             for h in range(halves):
-                nc.tensor.matmul(bank[:], weights[:, h, :], z_chunk[:, h, :], start=h == 0, stop=h == halves - 1)
-            columns = table[:, c * CHUNK : (c + 1) * CHUNK]
-            if c % 2 == 0:
+                nc.tensor.matmul(
+                    bank[:], weights[:, h, :], z_chunk[:, h, first : first + BLOCK], start=h == 0, stop=h == halves - 1
+                )
+            columns = table[:, b * BLOCK : (b + 1) * BLOCK]
+            if b % 2 == 0:
                 nc.scalar.copy(columns, bank[:])
             else:
                 nc.vector.tensor_copy(columns, bank[:])
 
-        for j in range(0, V, PIECE):
-            largest = own[:, j : j + PIECE]
-            for n in range(D):
-                first = (V * n + j) // 16
-                larger = held.tile([P, PIECE], F32, name=f"larger{j}_{n}")
+        largest = own
+        for n in range(D):
+            larger = [held.tile([P, PIECE], F32, name=f"larger{n}_{j}") for j in range(V // PIECE)]
+            for j in range(V // PIECE):
+                first = (V * n + PIECE * j) // 16
                 nc.vector.tensor_tensor(
-                    larger[:], table[:].indirect(offsets[:, first : first + PIECE // 16]), largest, MAX
+                    larger[j][:], table[:].indirect(offsets[:, first : first + PIECE // 16]), largest[j][:], MAX
                 )
-                largest = larger[:]
-            nc.sync.dma_start(out[:, j : j + PIECE], largest)
+            largest = larger
+        half = PIECE // 2
+        for j in range(V // PIECE):
+            middle = j * PIECE + half
+            nc.sync.dma_start(out[:, middle - half : middle], largest[j][:, :half])
+            nc.scalar.dma_start(out[:, middle : middle + half], largest[j][:, half:])

@@ -35,12 +35,10 @@ def tile_lookup_pjmax_out_kernel(tc, z, wt, x0, offs, out):
 
         nc.scalar.dma_start(weights[:], wt_by_feature)
         for c, z_chunk in enumerate(z_chunks):
-            queue = nc.sync if c % 2 == 0 else nc.scalar
-            queue.dma_start(z_chunk[:], z_by_feature[:, :, c * LOAD : (c + 1) * LOAD])
+            nc.sync.dma_start(z_chunk[:], z_by_feature[:, :, c * LOAD : (c + 1) * LOAD])
         nc.sync.dma_start(offsets[:], offs)
         for j, own_part in enumerate(own):
-            queue = nc.scalar if j % 2 == 0 else nc.sync
-            queue.dma_start(own_part[:], x0[:, j * PIECE : (j + 1) * PIECE])
+            nc.sync.dma_start(own_part[:], x0[:, j * PIECE : (j + 1) * PIECE])
 
         nc.gpsimd.memset(zeros[:], 0.0)
         for w in range(WARM_UPS):
@@ -55,9 +53,9 @@ def tile_lookup_pjmax_out_kernel(tc, z, wt, x0, offs, out):
                 )
             columns = table[:, b * BLOCK : (b + 1) * BLOCK]
             if b % 2 == 0:
-                nc.scalar.copy(columns, bank[:])
-            else:
                 nc.vector.tensor_copy(columns, bank[:])
+            else:
+                nc.scalar.copy(columns, bank[:])
 
         largest = own
         for n in range(D):

@@ -57,17 +57,13 @@ def tile_lookup_pjmax_out_kernel(tc, z, wt, x0, offs, out):
             else:
                 nc.scalar.copy(columns, bank[:])
 
-        largest = own
-        for n in range(D):
-            larger = [held.tile([P, PIECE], F32, name=f"larger{n}_{j}") for j in range(V // PIECE)]
-            for j in range(V // PIECE):
+        for j, own_part in enumerate(own):
+            largest = own_part
+            for n in range(D):
                 first = (V * n + PIECE * j) // 16
+                larger = held.tile([P, PIECE], F32, name=f"larger{j}_{n}")
                 nc.vector.tensor_tensor(
-                    larger[j][:], table[:].indirect(offsets[:, first : first + PIECE // 16]), largest[j][:], MAX
+                    larger[:], table[:].indirect(offsets[:, first : first + PIECE // 16]), largest[:], MAX
                 )
-            largest = larger
-        half = PIECE // 2
-        for j in range(V // PIECE):
-            middle = j * PIECE + half
-            nc.sync.dma_start(out[:, middle - half : middle], largest[j][:, :half])
-            nc.scalar.dma_start(out[:, middle : middle + half], largest[j][:, half:])
+                largest = larger
+            nc.sync.dma_start(out[:, j * PIECE : (j + 1) * PIECE], largest[:])

import concourse.mybir as mybir

P = 128
K = 256
S = 2048
V = 1024
D = 2
LOAD = 512
BLOCK = 256
PIECE = 512
WARM_UPS = 16
FLOPS = 2 * P * K * S

BF16, F32, U16 = mybir.dt.bfloat16, mybir.dt.float32, mybir.dt.uint16
MAX = mybir.AluOpType.max


def tile_lookup_pjmax_out_kernel(tc, z, wt, x0, offs, out):
    nc = tc.nc
    halves = K // P
    z_by_feature = z.rearrange("(p c) s -> p c s", c=halves)
    wt_by_feature = wt.rearrange("(p c) r -> p c r", c=halves)

    with (
        tc.tile_pool(name="held", bufs=1) as held,
        tc.psum_pool(name="psum", bufs=1) as psum,
    ):
        offsets = held.tile([P, D * V // 16], U16, name="offsets")
        weights = held.tile([P, halves, P], BF16, name="weights")
        table = held.tile([P, S], F32, name="table")
        own = [held.tile([P, PIECE], F32, name=f"own{j}") for j in range(V // PIECE)]
        zeros = held.tile([P, P], BF16, name="zeros")
        z_chunks = [held.tile([P, halves, LOAD], BF16, name=f"z_chunk{c}") for c in range(S // LOAD)]
        banks = [psum.tile([P, BLOCK], F32, name=f"bank{b}") for b in range(S // BLOCK)]

        nc.scalar.dma_start(weights[:], wt_by_feature)
        for c, z_chunk in enumerate(z_chunks):
            nc.sync.dma_start(z_chunk[:], z_by_feature[:, :, c * LOAD : (c + 1) * LOAD])
        nc.sync.dma_start(offsets[:], offs)
        for j, own_part in enumerate(own):
            nc.sync.dma_start(own_part[:], x0[:, j * PIECE : (j + 1) * PIECE])

        nc.gpsimd.memset(zeros[:], 0.0)
        for w in range(WARM_UPS):
            nc.tensor.matmul(banks[-1][:, :P], zeros[:], zeros[:], start=True, stop=True)

        for b, bank in enumerate(banks):
            z_chunk = z_chunks[b * BLOCK // LOAD]
            first = b * BLOCK % LOAD
            for h in range(halves):
                nc.tensor.matmul(
                    bank[:], weights[:, h, :], z_chunk[:, h, first : first + BLOCK], start=h == 0, stop=h == halves - 1
                )
            columns = table[:, b * BLOCK : (b + 1) * BLOCK]
            if b % 2 == 0:
                nc.vector.tensor_copy(columns, bank[:])
            else:
                nc.scalar.copy(columns, bank[:])

        for j, own_part in enumerate(own):
            largest = own_part
            for n in range(D):
                first = (V * n + PIECE * j) // 16
                larger = held.tile([P, PIECE], F32, name=f"larger{j}_{n}")
                nc.vector.tensor_tensor(
                    larger[:], table[:].indirect(offsets[:, first : first + PIECE // 16]), largest[:], MAX
                )
                largest = larger
            nc.sync.dma_start(out[:, j * PIECE : (j + 1) * PIECE], largest[:])
